import numpy as np, ml_dtypes
CORES = [40,41,42,43,44,45,46,47]
N = 8
BF = ml_dtypes.bfloat16
def gentries(a):
    return np.ascontiguousarray(a.reshape(8, 16, -1).transpose(0, 2, 1)).reshape(8, -1)
def gtable(e):
    e = np.asarray(e); return np.ascontiguousarray(e.reshape(8, -1, 16).transpose(0, 2, 1)).reshape(128, -1).astype(np.int32)
S, CAP, H = 2560, 384, 2
def channel(rng):
    v = rng.integers(-45, 46, (N, 128, S)) + rng.integers(-24, -4, (N, 128, 1))
    return np.clip(v, -63, 63).astype(np.float32).astype(BF)
def counts(rng):
    n = np.full((N, N), S // N, np.int64)
    for i in range(4 * N):
        q = rng.choice(N, 2, replace=False); r = rng.choice(N, 2, replace=False)
        d = min(CAP - n[q[0], r[0]], CAP - n[q[1], r[1]], n[q[0], r[1]], n[q[1], r[0]], (CAP - S // N) // 3 + 1)
        d = rng.integers(0, d + 1); n[q[0], r[0]] += d; n[q[1], r[1]] += d; n[q[0], r[1]] -= d; n[q[1], r[0]] -= d
    return n
def slots(rng, n, runs=False):
    sa = np.zeros((N, 8, S), np.int32); sb = np.zeros((N, 8, S), np.int32)
    def places():
        return rng.permutation(S) if not runs else np.arange(S) if rng.integers(0, 2) else np.arange(S)[::-1]
    for g in range(8):
        pa = [places() for q in range(N)]; pb = [places() for r in range(N)]
        for q in range(N):
            for r in range(N):
                m = int(n[g][q, r]); i = int(np.sum(n[g][q, :r])); j = int(np.sum(n[g][:q, r]))
                c = np.arange(m) if runs else rng.permutation(CAP)[:m]
                sa[q, g, pa[q][i:i + m]] = r * CAP + c; sb[r, g, pb[r][j:j + m]] = q * CAP + c
    return {"sa": np.stack([gtable(v) for v in sa]), "sb": np.stack([gtable(v) for v in sb])}
def setup_inputs(rng):
    d = {"a": channel(rng), "b": channel(rng)}
    d.update(slots(rng, [counts(rng) for g in range(8)])); return d
def setup_inputs_full(rng):
    d = setup_inputs(rng); n = np.full((8, N, N), S // N, np.int64); q = np.arange(N)
    for g in range(8):
        k = rng.integers(1, N); l = (k + rng.integers(1, N)) % N
        n[g, q, (q + k) % N] += CAP - S // N; n[g, q, (q + l) % N] -= CAP - S // N
    d.update(slots(rng, n)); return d
def setup_inputs_runs(rng):
    d = setup_inputs(rng); d.update(slots(rng, [counts(rng) for g in range(8)], True)); return d
def setup_inputs_ends(rng):
    d = setup_inputs(rng); vals = np.array([-63, -63, -63, -63, -15, -1, 0, 1, 15, 63]); k = rng.permutation(128)
    for name in ("a", "b"):
        v = rng.choice(vals, (N, 128, S)); v[:, k[:64]] = np.repeat(rng.choice(vals, (N, 64, S // 32)), 32, axis=2)
        v[:, k[0]] = 63; v[:, k[1]] = -63; v[:, k[2]] = 0
        d[name] = v.astype(np.float32).astype(BF)
    return d
def setup_inputs_spread(rng):
    d = setup_inputs(rng)
    for name in ("a", "b"):
        amp = 2 ** rng.integers(0, 7, (N, 1, S)) - 1
        v = np.minimum(np.floor(rng.random((N, 128, S)) ** 3 * (2 * amp + 1)), 2 * amp) - amp
        d[name] = v.astype(np.float32).astype(BF)
    return d
def check_inputs(d):
    bad = []
    try:
        for k in ("a", "b"):
            v = np.asarray(d[k]).astype(np.float64)
            if v.shape != (N, 128, S) or not np.isfinite(v).all() or (v != np.floor(v)).any() or (np.abs(v) > 63).any(): bad.append(k)
        used = []
        for k in ("sa", "sb"):
            v = np.asarray(d[k])
            if v.shape != (N, 128, S // 16) or v.min() < 0 or v.max() >= N * CAP:
                bad.append(k); continue
            u = np.zeros((N, 8, N * CAP), bool)
            for r in range(N): u[r][np.arange(8)[:, None], gentries(v[r])] = True
            if (np.sum(u, axis=-1) != S).any(): bad.append(k + " repeats")
            used.append(u.reshape(N, 8, N, CAP))
        if len(used) == 2 and (used[0] != used[1].transpose(2, 1, 0, 3)).any(): bad.append("slots of pairs")
    except Exception:
        bad.append("inputs")
    return bad
def partners(sa, sb):
    g = np.arange(8)[:, None]; inv = np.zeros((N, 8, N * CAP), np.int64); src = np.zeros((8, N * S), np.int64)
    for q in range(N): inv[q][g, gentries(sa[q])] = np.arange(S)
    for r in range(N):
        s = gentries(sb[r]).astype(np.int64); q = s // CAP
        src[:, r * S:(r + 1) * S] = q * S + inv[q, g, r * CAP + s - q * CAP]
    return src
def carry(e, src, back):
    x = np.ascontiguousarray(e.reshape(N, 8, 16, S).transpose(1, 2, 0, 3)).reshape(8, 16, N * S); z = np.zeros_like(x)
    for g in range(8):
        if back: z[g][:, src[g]] = x[g]
        else: z[g] = x[g][:, src[g]]
    return np.ascontiguousarray(z.reshape(8, 16, N, S).transpose(2, 0, 1, 3)).reshape(N, 128, S)
def scan(v, back):
    x = np.ascontiguousarray(np.moveaxis(v, -1, 0)); z = np.zeros_like(x); s = np.zeros_like(x[0])
    for t in (range(S - 1, -1, -1) if back else range(S)):
        s = np.maximum(s + x[t], 0); z[t] = s
    return np.moveaxis(z, 0, -1)
def extrinsic(v):
    e = np.full(v.shape, -15, np.int64)
    e[..., 1:] += np.minimum(scan(v, False), 15)[..., :-1]
    e[..., :-1] += np.minimum(scan(v, True), 15)[..., 1:]
    return e
def reference(a, b, sa, sb):
    src = partners(sa, sb)
    ca = a.astype(np.float32).astype(np.int64); cb = b.astype(np.float32).astype(np.int64)
    prior = np.zeros((N, 128, S), np.int64)
    for h in range(H // 2):
        prior = carry(extrinsic(ca + prior), src, False)
        prior = carry(extrinsic(cb + prior), src, True)
    return {"y": (ca + prior).astype(np.float32).astype(BF)}

@@ -1,0 +1,294 @@
+from concourse.bass import DstId, RemoteDMATransfer
+from concourse.mybir import AluOpType as ALU, ActivationFunctionType as ACT
+
+N, S, CAP = 8, 2560, 384
+W = N * CAP
+KS, KW, KC = S // 16, W // 16, CAP // 16
+BASE = 32
+TOP = 15.0
+
+NV1 = 1056
+NA2 = 576
+NV2 = 384
+CAPS = (512, 1152)
+YV = (640, 512, 384)
+YS = (512, 512)
+
+SCRATCH = {
+    "al": ("sbuf", [128, S], "bfloat16"),
+    "bl": ("sbuf", [128, S], "bfloat16"),
+    "l2": ("sbuf", [128, S], "bfloat16"),
+    "yl": ("sbuf", [128, S], "bfloat16"),
+    "zero": ("sbuf", [128, S], "bfloat16"),
+    "ff": ("sbuf", [128, 2 * S], "bfloat16"),
+    "bb": ("sbuf", [128, 2 * S], "bfloat16"),
+    "u0": ("sbuf", [128, W], "bfloat16"),
+    "u1": ("sbuf", [128, W], "bfloat16"),
+    "send0": ("sbuf", [128, W], "bfloat16"),
+    "send1": ("sbuf", [128, W], "bfloat16"),
+    "recv0": ("sbuf", [128, W], "bfloat16"),
+    "recv1": ("sbuf", [128, W], "bfloat16"),
+    "vals": ("sbuf", [128, S], "float32"),
+    "win": ("sbuf", [128, 4 * W], "float32"),
+    "zt": ("sbuf", [128, 2 * KW], "float32"),
+    "red": ("sbuf", [128, 4 * KW], "float32"),
+    "mrg": ("sbuf", [128, 2 * KW], "float32"),
+    "inv": ("sbuf", [128, 2 * KW], "uint16"),
+    "lst": ("sbuf", [128, 2 * KS], "int32"),
+    "t1": ("sbuf", [128, 2 * KS], "int32"),
+    "t2": ("sbuf", [128, 2 * KS], "int32"),
+    "t3": ("sbuf", [128, 2 * KS], "int32"),
+    "pos": ("sbuf", [128, 2 * KS], "uint16"),
+    "l16": ("sbuf", [128, 2 * KS], "uint16"),
+}
+POOL = 120
+SEMAPHORES = ["arr0", "arr1", "sent"] + ["e%d" % i for i in range(POOL)]
+
+
+def bits(engines):
+    m = 0
+    for e in engines:
+        m |= 1 << e
+    return m
+
+
+def rank_program(g, core, T, topo):
+    rank = T.rank_of(core)
+    if rank is None:
+        return
+    V, A, Y = g.vector, g.scalar, g.sync
+    names = {}
+
+    def sem(name):
+        if name not in names:
+            names[name] = T.sem["e%d" % len(names)]
+        return names[name]
+
+    def done(ins, name):
+        ins.then_inc(sem(name), 1)
+
+    def dma(ins, name):
+        ins.then_inc(sem(name), 16)
+
+    def wait(q, *ns):
+        for n in ns:
+            q.wait_ge(sem(n), 1)
+
+    def waitd(q, *ns):
+        for n in ns:
+            q.wait_ge(sem(n), 16)
+
+    near = [r for r in range(N) if topo.die(T.cores[r]) == topo.die(core)]
+    far = [r for r in range(N) if r not in near]
+    k = near.index(rank)
+    near = [near[(k + i) % len(near)] for i in range(1, len(near))]
+    far = [far[(k + i) % len(far)] for i in range(len(far))]
+
+    def grouping(first_single):
+        c, s = list(far), list(near)
+        out = []
+        if first_single:
+            out.append([c.pop(0)])
+        else:
+            out.append([c.pop(0), c.pop(0)])
+        while c and s:
+            out.append([c.pop(0), s.pop(0)])
+        for r in c + s:
+            out.append([r])
+        return out
+
+    groups = [grouping(True), grouping(False)]
+
+    def arrivals(h):
+        total = 0
+        for q in range(N):
+            if q == rank:
+                continue
+            total += counts_of(q, h)[rank]
+        return total
+
+    def counts_of(q, h):
+        cq = T.cores[q]
+        nr = [r for r in range(N) if topo.die(T.cores[r]) == topo.die(cq)]
+        fr = [r for r in range(N) if r not in nr]
+        kq = nr.index(q)
+        nr = [nr[(kq + i) % len(nr)] for i in range(1, len(nr))]
+        fr = [fr[(kq + i) % len(fr)] for i in range(len(fr))]
+        shape = [len(x) for x in groups[h]]
+        kinds = [[r in far for r in x] for x in groups[h]]
+        out = {}
+        for n, kk in zip(shape, kinds):
+            for isfar in kk:
+                r = fr.pop(0) if isfar else nr.pop(0)
+                out[r] = len(topo.engines(cq, T.cores[r])) // n
+        return out
+
+    blk = lambda t, r: t[:, r * CAP:(r + 1) * CAP]
+    lcol = lambda h, lo, hi: slice(h * KS + lo // 16, h * KS + hi // 16)
+    window = lambda i: T.win[:, i * W:(i + 1) * W]
+
+    dma(Y.dma_start(T.lst[:, 0:KS], T.sa[:]), "sa")
+    wait(Y, "zt")
+    dma(Y.dma_start(T.win[0:128:16, 0:2 * W], T.zt[:]), "init0")
+    dma(Y.dma_start(T.al[:], T.a[:]), "a")
+    dma(Y.dma_start(T.lst[:, KS:2 * KS], T.sb[:]), "sb")
+    dma(Y.dma_start(T.win[0:128:16, 2 * W:4 * W], T.zt[:]), "init1")
+
+    def relayout(i, *after):
+        wait(Y, *after)
+        dma(Y.dma_start(T.red[:, i * KW:(i + 1) * KW], T.win[0:128:16, i * W:(i + 1) * W]), "red%d" % i)
+
+    relayout(0, "scv0")
+    relayout(1, "sca0")
+    dma(Y.dma_start(T.bl[:], T.b[:]), "b")
+    relayout(2, "scv1")
+    relayout(3, "sca1a", "sca1b")
+    lo = 0
+    for i, n in enumerate(YV):
+        wait(Y, "yv%d" % i)
+        Y.dma_start(T.y[:, lo:lo + n], T.yl[:, lo:lo + n]).then_inc(sem("stored"), 16)
+        lo += n
+    Y.wait_ge(sem("stored"), 16 * len(YV))
+    ys0 = lo
+
+    done(g.iota(T.vals[:, 0:256], [[1, 256]], BASE, 0, allow_small_or_imprecise_dtypes=True), "v0")
+    done(g.iota(T.vals[:, 256:1280], [[1, 1024]], BASE + 256, 0, allow_small_or_imprecise_dtypes=True), "v1")
+    done(g.iota(T.zero[:, 0:S // 2], [[0, S // 2]], 0, 0, allow_small_or_imprecise_dtypes=True), "z0")
+    done(V.memset(T.zt[:], 0.0), "zt")
+    done(V.memset(T.ff[:, 0:2 * S:S], 0.0), "padf")
+    done(V.memset(T.bb[:, S - 1:2 * S:S], 0.0), "padb")
+    done(V.memset(T.zero[:, S // 2:S], 0.0), "z1")
+    wait(V, "v0")
+    for i in range(3):
+        c0 = 1280 + 256 * i
+        done(V.tensor_scalar(T.vals[:, c0:c0 + 256], T.vals[:, 0:256], float(c0), None, ALU.add), "vv%d" % i)
+    wait(A, "v0")
+    for i in range(2):
+        c0 = 2048 + 256 * i
+        done(A.activation(T.vals[:, c0:c0 + 256], T.vals[:, 0:256], ACT.Silu, bias=float(c0)), "va%d" % i)
+
+    def step(level, cs, name):
+        if level == 0:
+            ins = V.tensor_scalar(T.t1[:, cs], T.lst[:, cs], 15, None, ALU.bitwise_and)
+        elif level == 1:
+            ins = V.tensor_scalar(T.t2[:, cs], T.t1[:, cs], float(W - 1), None, ALU.mult)
+        elif level == 2:
+            ins = V.tensor_tensor(T.t3[:, cs], T.t2[:, cs], T.lst[:, cs], ALU.add)
+        else:
+            ins = V.tensor_scalar(T.pos[:, cs], T.t3[:, cs], 1.0 / 16, None, ALU.mult)
+        done(ins, "%s%d" % (name, level))
+
+    waitd(V, "sa")
+    for level in range(4):
+        for cs, name in ((lcol(0, NV1, S), "ps"), (lcol(0, 0, NV1), "pv")):
+            if level:
+                wait(V, "%s%d" % (name, level - 1))
+            step(level, cs, name)
+    wait(V, "v1", "pv3", "padf", "padb", "z1")
+    waitd(V, "init0")
+    done(V.tensor_copy(window(0).indirect(T.pos[:, lcol(0, 0, NV1)]), T.vals[:, 0:NV1]), "scv0")
+    cb = lcol(1, 0, S)
+    waitd(V, "sb")
+    step(0, cb, "pb")
+    done(V.tensor_copy(T.l16[:, 0:KS], T.lst[:, 0:KS]), "l16a")
+    wait(V, "pb0")
+    step(1, cb, "pb")
+    done(V.tensor_copy(T.l16[:, cb], T.lst[:, cb]), "l16b")
+    wait(V, "pb1")
+    step(2, cb, "pb")
+    wait(V, "pb2")
+    step(3, cb, "pb")
+
+    wait(A, "v1", "vv0", "vv1", "vv2", "va0", "va1", "ps3")
+    waitd(A, "init0")
+    done(A.activation(window(1).indirect(T.pos[:, lcol(0, NV1, S)]), T.vals[:, NV1:S], ACT.Silu), "sca0")
+    wait(A, "pb3")
+    waitd(A, "init1")
+    done(A.activation(window(3).indirect(T.pos[:, lcol(1, S - NA2, S)]), T.vals[:, S - NA2:S], ACT.Silu), "sca1a")
+
+    sent = [0]
+
+    def half(h, src):
+        o = h * S
+        F, B = T.ff[:, o:o + S], T.bb[:, o:o + S]
+        U, SEND, RECV = T["u%d" % h], T["send%d" % h], T["recv%d" % h]
+        back = slice(o + S - 2, o - 1 if o else None, -1)
+        done(V.tensor_tensor_scan(T.bb[:, back], src[:, S - 1:0:-1], T.zero[:, 0:S - 1], 0.0, ALU.add, ALU.max), "sb%d" % h)
+        done(V.tensor_tensor_scan(T.ff[:, o + 1:o + S], src[:, 0:S - 1], T.zero[:, 0:S - 1], 0.0, ALU.add, ALU.max), "sf%d" % h)
+        cuts = (0,) + CAPS + (S,)
+
+        def cap(i):
+            cs = slice(o + cuts[i], o + cuts[i + 1])
+            done(V.tensor_scalar(T.bb[:, cs], T.bb[:, cs], TOP, None, ALU.min), "cap%d%d" % (h, i))
+
+        mk = slice(h * KW, (h + 1) * KW)
+        wait(V, "sb%d" % h)
+        cap(0)
+        waitd(V, "red%d" % (2 * h), "red%d" % (2 * h + 1))
+        done(V.tensor_tensor(T.mrg[:, mk], T.red[:, 2 * h * KW:(2 * h + 1) * KW],
+                             T.red[:, (2 * h + 1) * KW:(2 * h + 2) * KW], ALU.max), "mrg%d" % h)
+        cap(1)
+        wait(V, "mrg%d" % h)
+        done(V.tensor_scalar(T.inv[:, mk], T.mrg[:, mk], 0.25 - BASE, 0.0, ALU.add, ALU.max), "inv%d" % h)
+        cap(2)
+        order = [r for x in groups[h] for r in x] + [rank]
+        off = lambda r: T.inv[:, h * KW + r * KC:h * KW + (r + 1) * KC]
+        wait(A, "inv%d" % h, "sf%d" % h)
+        for r in order:
+            done(A.activation(blk(U, r), F.indirect(off(r)), ACT.Relu, bias=TOP, scale=-1.0), "u%d%d" % (h, r))
+        wait(V, "inv%d" % h, "cap%d0" % h, "cap%d1" % h, "cap%d2" % h)
+        for r in order:
+            wait(V, "u%d%d" % (h, r))
+            out = blk(RECV, r) if r == rank else blk(SEND, r)
+            done(V.tensor_tensor(out, B.indirect(off(r)), blk(U, r), ALU.subtract), "e%d%d" % (h, r))
+        arr = T.sem["arr%d" % h]
+        for x in groups[h]:
+            for r in x:
+                wait(g, "e%d%d" % (h, r))
+            trs = []
+            for i, r in enumerate(x):
+                eng = topo.engines(core, T.cores[r])[i::len(x)]
+                rid, pid, _ = topo.addr(T.cores[r])
+                trs.append(RemoteDMATransfer(dst_ids=[DstId(rid=rid, pnc=pid)], dma_engine_mask=bits(eng),
+                                             remote_sem=arr, src=blk(SEND, r), dst=blk(RECV, rank)))
+                sent[0] += len(eng)
+            g.remote_dma_fused(trs, local_sem=T.sem.sent)
+
+    waitd(V, "a")
+    wait(V, "z0")
+    half(0, T.al)
+    wait(A, "sca1a")
+    done(A.activation(window(3).indirect(T.pos[:, lcol(1, NV2, S - NA2)]), T.vals[:, NV2:S - NA2], ACT.Silu), "sca1b")
+    wait(V, "pb3")
+    waitd(V, "init1")
+    done(V.tensor_copy(window(2).indirect(T.pos[:, lcol(1, 0, NV2)]), T.vals[:, 0:NV2]), "scv1")
+    if YS:
+        g.wait_ge(T.sem.sent, sent[0])
+        dma(g.dma_start(T.y[:, ys0:S], T.a[:, ys0:S]), "pre")
+
+    wait(V, "l16a", "l16b", "e0%d" % rank)
+    waitd(V, "b")
+    V.wait_ge(T.sem.arr0, arrivals(0))
+    done(V.tensor_tensor(T.l2[:], T.recv0[:, 0:W].indirect(T.l16[:, cb]), T.bl[:], ALU.add), "l2")
+    wait(V, "l2")
+    half(1, T.l2)
+
+    wait(V, "e1%d" % rank)
+    V.wait_ge(T.sem.arr1, arrivals(1))
+    lo = 0
+    for i, n in enumerate(YV):
+        done(V.tensor_tensor(T.yl[:, lo:lo + n], T.recv1[:, 0:W].indirect(T.l16[:, lcol(0, lo, lo + n)]),
+                             T.al[:, lo:lo + n], ALU.add), "yv%d" % i)
+        lo += n
+    if YS:
+        wait(A, "e1%d" % rank, "l16a")
+        A.wait_ge(T.sem.arr1, arrivals(1))
+        waitd(g, "pre")
+        for i, n in enumerate(YS):
+            done(A.activation(T.yl[:, lo:lo + n], T.recv1[:, 0:W].indirect(T.l16[:, lcol(0, lo, lo + n)]),
+                              ACT.Identity), "ya%d" % i)
+            wait(g, "ya%d" % i)
+            g.dma_start(T.y[:, lo:lo + n], T.yl[:, lo:lo + n], accum_op=ALU.add).then_inc(sem("added"), 16)
+            lo += n
+        g.wait_ge(sem("added"), 16 * len(YS))
+    g.wait_ge(T.sem.sent, sent[0])

@@ -7,42 +7,69 @@ KS, KW, KC = S // 16, W // 16, CAP // 16
 BASE = 32
 TOP = 15.0
 
-NV1 = 1056
-NA2 = 576
-NV2 = 384
-CAPS = (512, 1152)
-YV = (640, 512, 384)
-YS = (512, 512)
+LA = (448, 384)
+YV = (512, 640, 544)
+YS = (480, 384)
+CALLS = (("FFFFNNN",), ("FF", "FN", "F", "N", "N"))
+I0 = 64
+CUTS = (384, 1152, 1024)
+CAPA = ("f0", "f1", "b1", "f2", "b2")
+LOADS = (("sb", "a", "sa", "b", "init"), ())
+N1 = 0
+ZG = 1280
+LATE = True
+STEPS = ("0123", "", "a", "", "", "", "")
+INV = 1
+EVAC = 7
+SOLO = 5
+VCAP = 0
+FLIP_A = (1, 3, 5)
+PE = True
+STORES = "01a2"
+NH = 0
 
 SCRATCH = {
     "al": ("sbuf", [128, S], "bfloat16"),
     "bl": ("sbuf", [128, S], "bfloat16"),
     "l2": ("sbuf", [128, S], "bfloat16"),
+    "pl": ("sbuf", [128, S], "bfloat16"),
     "yl": ("sbuf", [128, S], "bfloat16"),
     "zero": ("sbuf", [128, S], "bfloat16"),
-    "ff": ("sbuf", [128, 2 * S], "bfloat16"),
-    "bb": ("sbuf", [128, 2 * S], "bfloat16"),
-    "u0": ("sbuf", [128, W], "bfloat16"),
-    "u1": ("sbuf", [128, W], "bfloat16"),
+    "fb": ("sbuf", [128, 4 * S], "bfloat16"),
+    "fc": ("sbuf", [128, S], "bfloat16"),
+    "uf": ("sbuf", [128, CAP], "bfloat16"),
+    "uu": ("sbuf", [128, W], "bfloat16"),
     "send0": ("sbuf", [128, W], "bfloat16"),
     "send1": ("sbuf", [128, W], "bfloat16"),
     "recv0": ("sbuf", [128, W], "bfloat16"),
     "recv1": ("sbuf", [128, W], "bfloat16"),
+    "ones": ("sbuf", [128, 128], "bfloat16"),
+    "ident": ("sbuf", [128, 128], "bfloat16"),
     "vals": ("sbuf", [128, S], "float32"),
-    "win": ("sbuf", [128, 4 * W], "float32"),
-    "zt": ("sbuf", [128, 2 * KW], "float32"),
-    "red": ("sbuf", [128, 4 * KW], "float32"),
-    "mrg": ("sbuf", [128, 2 * KW], "float32"),
-    "inv": ("sbuf", [128, 2 * KW], "uint16"),
+    "win": ("sbuf", [128, W], "float32"),
+    "wina": ("sbuf", [128, W], "float32"),
+    "reda": ("sbuf", [128, KW], "float32"),
+    "inva": ("sbuf", [128, KW], "uint16"),
+    "xd": ("sbuf", [128, 528], "bfloat16"),
+    "h1": ("sbuf", [128, 32], "int32"),
+    "h2": ("sbuf", [128, 32], "float32"),
+    "h3": ("sbuf", [128, 32], "float32"),
+    "posa": ("sbuf", [128, 32], "uint16"),
+    "zt": ("sbuf", [128, KW], "float32"),
+    "red": ("sbuf", [128, KW], "float32"),
+    "inv": ("sbuf", [128, KW], "uint16"),
     "lst": ("sbuf", [128, 2 * KS], "int32"),
-    "t1": ("sbuf", [128, 2 * KS], "int32"),
-    "t2": ("sbuf", [128, 2 * KS], "int32"),
-    "t3": ("sbuf", [128, 2 * KS], "int32"),
-    "pos": ("sbuf", [128, 2 * KS], "uint16"),
+    "t1": ("sbuf", [128, KS], "int32"),
+    "t2": ("sbuf", [128, KS], "float32"),
+    "t3": ("sbuf", [128, KS], "float32"),
+    "pos": ("sbuf", [128, KS], "uint16"),
     "l16": ("sbuf", [128, 2 * KS], "uint16"),
+    "sum0": ("psum", [128, 512], "float32"),
+    "sum1": ("psum", [128, 512], "float32"),
+    "sum2": ("psum", [128, 512], "float32"),
 }
 POOL = 120
-SEMAPHORES = ["arr0", "arr1", "sent"] + ["e%d" % i for i in range(POOL)]
+SEMAPHORES = ["arr0", "sent"] + ["arr1%d" % i for i in range(N)] + ["e%d" % i for i in range(POOL)]
 
 
 def bits(engines):
@@ -56,7 +83,7 @@ def rank_program(g, core, T, topo):
     rank = T.rank_of(core)
     if rank is None:
         return
-    V, A, Y = g.vector, g.scalar, g.sync
+    V, A, Y, P = g.vector, g.scalar, g.sync, g.tensor
     names = {}
 
     def sem(name):
@@ -78,217 +105,350 @@ def rank_program(g, core, T, topo):
         for n in ns:
             q.wait_ge(sem(n), 16)
 
-    near = [r for r in range(N) if topo.die(T.cores[r]) == topo.die(core)]
-    far = [r for r in range(N) if r not in near]
-    k = near.index(rank)
-    near = [near[(k + i) % len(near)] for i in range(1, len(near))]
-    far = [far[(k + i) % len(far)] for i in range(len(far))]
+    def calls_of(q, h):
+        cq = T.cores[q]
+        near = [r for r in range(N) if topo.die(T.cores[r]) == topo.die(cq)]
+        far = [r for r in range(N) if r not in near]
+        k = near.index(q)
+        near = [near[(k + i) % len(near)] for i in range(1, len(near))]
+        far = [far[(k + i) % len(far)] for i in range(len(far))]
+        engines = lambda r: topo.engines(cq, T.cores[r])
 
-    def grouping(first_single):
-        c, s = list(far), list(near)
+        def deal(ranks, pick):
+            n = 1 << (len(ranks) - 1).bit_length()
+            share = lambda r, js: [e for j in js for e in pick(engines(r))[j::n]]
+            extra = n - len(ranks)
+            return [(r, share(r, (i, n - 1 - i) if i < extra else (i,))) for i, r in enumerate(ranks)]
+
         out = []
-        if first_single:
-            out.append([c.pop(0)])
-        else:
-            out.append([c.pop(0), c.pop(0)])
-        while c and s:
-            out.append([c.pop(0), s.pop(0)])
-        for r in c + s:
-            out.append([r])
+        for kinds in CALLS[h]:
+            rs = [far.pop(0) if c in "Ff" else near.pop(0) for c in kinds]
+            fs = [r for r, c in zip(rs, kinds) if c in "Ff"]
+            ns = [r for r, c in zip(rs, kinds) if c in "Nn"]
+            half = (fs and ns) or kinds.islower()
+            dealt = dict((deal(fs, lambda e: e[0::2] if half else e) if fs else []) +
+                         (deal(ns, lambda e: e[1::2] if half else e) if ns else []))
+            out.append([(r, dealt[r]) for r in rs])
         return out
-
-    groups = [grouping(True), grouping(False)]
 
     def arrivals(h):
-        total = 0
-        for q in range(N):
-            if q == rank:
-                continue
-            total += counts_of(q, h)[rank]
-        return total
-
-    def counts_of(q, h):
-        cq = T.cores[q]
-        nr = [r for r in range(N) if topo.die(T.cores[r]) == topo.die(cq)]
-        fr = [r for r in range(N) if r not in nr]
-        kq = nr.index(q)
-        nr = [nr[(kq + i) % len(nr)] for i in range(1, len(nr))]
-        fr = [fr[(kq + i) % len(fr)] for i in range(len(fr))]
-        shape = [len(x) for x in groups[h]]
-        kinds = [[r in far for r in x] for x in groups[h]]
-        out = {}
-        for n, kk in zip(shape, kinds):
-            for isfar in kk:
-                r = fr.pop(0) if isfar else nr.pop(0)
-                out[r] = len(topo.engines(cq, T.cores[r])) // n
-        return out
+        return sum(len(e) for q in range(N) if q != rank for x in calls_of(q, h) for r, e in x if r == rank)
 
     blk = lambda t, r: t[:, r * CAP:(r + 1) * CAP]
     lcol = lambda h, lo, hi: slice(h * KS + lo // 16, h * KS + hi // 16)
-    window = lambda i: T.win[:, i * W:(i + 1) * W]
-
-    dma(Y.dma_start(T.lst[:, 0:KS], T.sa[:]), "sa")
-    wait(Y, "zt")
-    dma(Y.dma_start(T.win[0:128:16, 0:2 * W], T.zt[:]), "init0")
-    dma(Y.dma_start(T.al[:], T.a[:]), "a")
-    dma(Y.dma_start(T.lst[:, KS:2 * KS], T.sb[:]), "sb")
-    dma(Y.dma_start(T.win[0:128:16, 2 * W:4 * W], T.zt[:]), "init1")
-
-    def relayout(i, *after):
-        wait(Y, *after)
-        dma(Y.dma_start(T.red[:, i * KW:(i + 1) * KW], T.win[0:128:16, i * W:(i + 1) * W]), "red%d" % i)
-
-    relayout(0, "scv0")
-    relayout(1, "sca0")
-    dma(Y.dma_start(T.bl[:], T.b[:]), "b")
-    relayout(2, "scv1")
-    relayout(3, "sca1a", "sca1b")
-    lo = 0
-    for i, n in enumerate(YV):
-        wait(Y, "yv%d" % i)
-        Y.dma_start(T.y[:, lo:lo + n], T.yl[:, lo:lo + n]).then_inc(sem("stored"), 16)
-        lo += n
-    Y.wait_ge(sem("stored"), 16 * len(YV))
-    ys0 = lo
-
-    done(g.iota(T.vals[:, 0:256], [[1, 256]], BASE, 0, allow_small_or_imprecise_dtypes=True), "v0")
-    done(g.iota(T.vals[:, 256:1280], [[1, 1024]], BASE + 256, 0, allow_small_or_imprecise_dtypes=True), "v1")
-    done(g.iota(T.zero[:, 0:S // 2], [[0, S // 2]], 0, 0, allow_small_or_imprecise_dtypes=True), "z0")
-    done(V.memset(T.zt[:], 0.0), "zt")
-    done(V.memset(T.ff[:, 0:2 * S:S], 0.0), "padf")
-    done(V.memset(T.bb[:, S - 1:2 * S:S], 0.0), "padb")
-    done(V.memset(T.zero[:, S // 2:S], 0.0), "z1")
-    wait(V, "v0")
-    for i in range(3):
-        c0 = 1280 + 256 * i
-        done(V.tensor_scalar(T.vals[:, c0:c0 + 256], T.vals[:, 0:256], float(c0), None, ALU.add), "vv%d" % i)
-    wait(A, "v0")
-    for i in range(2):
-        c0 = 2048 + 256 * i
-        done(A.activation(T.vals[:, c0:c0 + 256], T.vals[:, 0:256], ACT.Silu, bias=float(c0)), "va%d" % i)
-
-    def step(level, cs, name):
-        if level == 0:
-            ins = V.tensor_scalar(T.t1[:, cs], T.lst[:, cs], 15, None, ALU.bitwise_and)
-        elif level == 1:
-            ins = V.tensor_scalar(T.t2[:, cs], T.t1[:, cs], float(W - 1), None, ALU.mult)
-        elif level == 2:
-            ins = V.tensor_tensor(T.t3[:, cs], T.t2[:, cs], T.lst[:, cs], ALU.add)
-        else:
-            ins = V.tensor_scalar(T.pos[:, cs], T.t3[:, cs], 1.0 / 16, None, ALU.mult)
-        done(ins, "%s%d" % (name, level))
-
-    waitd(V, "sa")
-    for level in range(4):
-        for cs, name in ((lcol(0, NV1, S), "ps"), (lcol(0, 0, NV1), "pv")):
-            if level:
-                wait(V, "%s%d" % (name, level - 1))
-            step(level, cs, name)
-    wait(V, "v1", "pv3", "padf", "padb", "z1")
-    waitd(V, "init0")
-    done(V.tensor_copy(window(0).indirect(T.pos[:, lcol(0, 0, NV1)]), T.vals[:, 0:NV1]), "scv0")
-    cb = lcol(1, 0, S)
-    waitd(V, "sb")
-    step(0, cb, "pb")
-    done(V.tensor_copy(T.l16[:, 0:KS], T.lst[:, 0:KS]), "l16a")
-    wait(V, "pb0")
-    step(1, cb, "pb")
-    done(V.tensor_copy(T.l16[:, cb], T.lst[:, cb]), "l16b")
-    wait(V, "pb1")
-    step(2, cb, "pb")
-    wait(V, "pb2")
-    step(3, cb, "pb")
-
-    wait(A, "v1", "vv0", "vv1", "vv2", "va0", "va1", "ps3")
-    waitd(A, "init0")
-    done(A.activation(window(1).indirect(T.pos[:, lcol(0, NV1, S)]), T.vals[:, NV1:S], ACT.Silu), "sca0")
-    wait(A, "pb3")
-    waitd(A, "init1")
-    done(A.activation(window(3).indirect(T.pos[:, lcol(1, S - NA2, S)]), T.vals[:, S - NA2:S], ACT.Silu), "sca1a")
-
+    ca, cb = lcol(0, 0, S), lcol(1, 0, S)
+    rows = T.win[0:128:16, :]
     sent = [0]
 
-    def half(h, src):
-        o = h * S
-        F, B = T.ff[:, o:o + S], T.bb[:, o:o + S]
-        U, SEND, RECV = T["u%d" % h], T["send%d" % h], T["recv%d" % h]
-        back = slice(o + S - 2, o - 1 if o else None, -1)
-        done(V.tensor_tensor_scan(T.bb[:, back], src[:, S - 1:0:-1], T.zero[:, 0:S - 1], 0.0, ALU.add, ALU.max), "sb%d" % h)
-        done(V.tensor_tensor_scan(T.ff[:, o + 1:o + S], src[:, 0:S - 1], T.zero[:, 0:S - 1], 0.0, ALU.add, ALU.max), "sf%d" % h)
-        cuts = (0,) + CAPS + (S,)
+    def send(call, src, dst, arr):
+        trs = []
+        for r, eng in call:
+            rid, pid, _ = topo.addr(T.cores[r])
+            trs.append(RemoteDMATransfer(dst_ids=[DstId(rid=rid, pnc=pid)], dma_engine_mask=bits(eng),
+                                         remote_sem=arr, src=blk(src, r), dst=blk(dst, rank)))
+            sent[0] += len(eng)
+        g.remote_dma_fused(trs, local_sem=T.sem.sent)
 
-        def cap(i):
-            cs = slice(o + cuts[i], o + cuts[i + 1])
-            done(V.tensor_scalar(T.bb[:, cs], T.bb[:, cs], TOP, None, ALU.min), "cap%d%d" % (h, i))
-
-        mk = slice(h * KW, (h + 1) * KW)
-        wait(V, "sb%d" % h)
-        cap(0)
-        waitd(V, "red%d" % (2 * h), "red%d" % (2 * h + 1))
-        done(V.tensor_tensor(T.mrg[:, mk], T.red[:, 2 * h * KW:(2 * h + 1) * KW],
-                             T.red[:, (2 * h + 1) * KW:(2 * h + 2) * KW], ALU.max), "mrg%d" % h)
-        cap(1)
-        wait(V, "mrg%d" % h)
-        done(V.tensor_scalar(T.inv[:, mk], T.mrg[:, mk], 0.25 - BASE, 0.0, ALU.add, ALU.max), "inv%d" % h)
-        cap(2)
-        order = [r for x in groups[h] for r in x] + [rank]
-        off = lambda r: T.inv[:, h * KW + r * KC:h * KW + (r + 1) * KC]
-        wait(A, "inv%d" % h, "sf%d" % h)
-        for r in order:
-            done(A.activation(blk(U, r), F.indirect(off(r)), ACT.Relu, bias=TOP, scale=-1.0), "u%d%d" % (h, r))
-        wait(V, "inv%d" % h, "cap%d0" % h, "cap%d1" % h, "cap%d2" % h)
-        for r in order:
-            wait(V, "u%d%d" % (h, r))
-            out = blk(RECV, r) if r == rank else blk(SEND, r)
-            done(V.tensor_tensor(out, B.indirect(off(r)), blk(U, r), ALU.subtract), "e%d%d" % (h, r))
-        arr = T.sem["arr%d" % h]
-        for x in groups[h]:
-            for r in x:
-                wait(g, "e%d%d" % (h, r))
-            trs = []
-            for i, r in enumerate(x):
-                eng = topo.engines(core, T.cores[r])[i::len(x)]
-                rid, pid, _ = topo.addr(T.cores[r])
-                trs.append(RemoteDMATransfer(dst_ids=[DstId(rid=rid, pnc=pid)], dma_engine_mask=bits(eng),
-                                             remote_sem=arr, src=blk(SEND, r), dst=blk(RECV, rank)))
-                sent[0] += len(eng)
-            g.remote_dma_fused(trs, local_sem=T.sem.sent)
-
-    waitd(V, "a")
-    wait(V, "z0")
-    half(0, T.al)
-    wait(A, "sca1a")
-    done(A.activation(window(3).indirect(T.pos[:, lcol(1, NV2, S - NA2)]), T.vals[:, NV2:S - NA2], ACT.Silu), "sca1b")
-    wait(V, "pb3")
-    waitd(V, "init1")
-    done(V.tensor_copy(window(2).indirect(T.pos[:, lcol(1, 0, NV2)]), T.vals[:, 0:NV2]), "scv1")
-    if YS:
-        g.wait_ge(T.sem.sent, sent[0])
-        dma(g.dma_start(T.y[:, ys0:S], T.a[:, ys0:S]), "pre")
-
-    wait(V, "l16a", "l16b", "e0%d" % rank)
-    waitd(V, "b")
-    V.wait_ge(T.sem.arr0, arrivals(0))
-    done(V.tensor_tensor(T.l2[:], T.recv0[:, 0:W].indirect(T.l16[:, cb]), T.bl[:], ALU.add), "l2")
-    wait(V, "l2")
-    half(1, T.l2)
-
-    wait(V, "e1%d" % rank)
-    V.wait_ge(T.sem.arr1, arrivals(1))
-    lo = 0
-    for i, n in enumerate(YV):
-        done(V.tensor_tensor(T.yl[:, lo:lo + n], T.recv1[:, 0:W].indirect(T.l16[:, lcol(0, lo, lo + n)]),
-                             T.al[:, lo:lo + n], ALU.add), "yv%d" % i)
-        lo += n
-    if YS:
-        wait(A, "e1%d" % rank, "l16a")
-        A.wait_ge(T.sem.arr1, arrivals(1))
-        waitd(g, "pre")
-        for i, n in enumerate(YS):
-            done(A.activation(T.yl[:, lo:lo + n], T.recv1[:, 0:W].indirect(T.l16[:, lcol(0, lo, lo + n)]),
-                              ACT.Identity), "ya%d" % i)
-            wait(g, "ya%d" % i)
-            g.dma_start(T.y[:, lo:lo + n], T.yl[:, lo:lo + n], accum_op=ALU.add).then_inc(sem("added"), 16)
+    def pieces(lo, sizes):
+        out = []
+        for n in sizes:
+            out.append((lo, lo + n))
             lo += n
+        return out
+
+    loads = {"sb": T.lst[:, cb], "sa": T.lst[:, ca], "a": T.al[:], "b": T.bl[:]}
+    for Q, which in zip((Y, A), LOADS):
+        for name in which:
+            if name == "init":
+                wait(Q, "zt")
+                dma(Q.dma_start(rows, T.zt[:]), "init")
+            else:
+                dma(Q.dma_start(loads[name], T[name][:]), name)
+    if NH:
+        wait(Y, "sca")
+        dma(Y.dma_start(T.reda[:], T.wina[0:128:16, :]), "reda")
+    wait(Y, "scb")
+    if LATE:
+        Y.wait_ge(T.sem.sent, sum(len(e) for x in calls_of(rank, 0) for r, e in x))
+    dma(Y.dma_start(T.red[:], rows), "red")
+    for c in STORES:
+        i = int(c) if c.isdigit() else "abc".index(c)
+        lo, hi = pieces(0, YV)[i] if c.isdigit() else pieces(sum(YV), YS)[i]
+        wait(Y, ("yv%d" if c.isdigit() else "yb%d") % i)
+        Y.dma_start(T.y[:, lo:hi], T.yl[:, lo:hi]).then_inc(sem("stored"), 16)
+    Y.wait_ge(sem("stored"), 16 * (len(YV) + (len(YS) if PE else 0)))
+
+    def iota(out, step, base, name):
+        done(g.iota(out, [[step, out.shape[1]]], base, 0, allow_small_or_imprecise_dtypes=True), name)
+
+    iota(T.vals[:, 0:I0], 1, BASE, "v0")
+    if NH:
+        done(V.memset(T.zt[:], 0.0), "zt")
+        done(V.memset(T.xd[:, 0:16], 0.0), "xpad")
+        wait(A, "zt")
+        dma(A.dma_start(T.wina[0:128:16, :], T.zt[:]), "inita")
+        iota(T.vals[:, I0:NH], 1, BASE + I0, "vh")
+        iota(T.vals[:, NH:S - I0], 1, BASE + NH, "v1")
+    elif N1:
+        done(V.memset(T.zt[:], 0.0), "zt")
+        iota(T.vals[:, I0:N1], 1, BASE + I0, "vh")
+        iota(T.vals[:, N1:S - I0], 1, BASE + N1, "v1")
+    else:
+        iota(T.vals[:, I0:S - I0], 1, BASE + I0, "v1")
+        iota(T.zt[:], 0, 0, "zt")
+    iota(T.ones[:], 0, 1, "ones")
+    wait(g, "ones")
+    done(g.affine_select(T.ident[:], T.ones[:], [[-1, 128]], ALU.is_equal, 0.0, 0, 1), "ident")
+    iota(T.zero[:, 0:ZG], 0, 0, "zero")
+    done(V.memset(T.send0[:], -TOP), "clear")
+    done(V.memset(T.fb[:, 0:2 * S:2 * S - 1], -TOP), "pad0")
+    wait(A, "v0")
+    done(A.activation(T.vals[:, S - I0:S], T.vals[:, 0:I0], ACT.Silu, bias=float(S - I0)), "va")
+
+    wait(V, "pad0", "clear")
+    hs = slice(0, NH // 16)
+
+    def steps(which):
+        for c in which:
+            if c == "0":
+                waitd(V, "sb")
+                done(V.tensor_scalar(T.t1[:], T.lst[:, cb], 15, None, ALU.bitwise_and), "p0")
+            elif c == "1":
+                wait(V, "p0")
+                done(V.tensor_scalar(T.t2[:], T.t1[:], float(W - 1), None, ALU.mult), "p1")
+            elif c == "2":
+                wait(V, "p1")
+                done(V.tensor_tensor(T.t3[:], T.t2[:], T.lst[:, cb], ALU.add), "p2")
+            elif c == "3":
+                wait(V, "p2")
+                done(V.tensor_scalar(T.pos[:], T.t3[:], 1.0 / 16, None, ALU.mult), "p3")
+            elif c == "A":
+                waitd(V, "sa")
+                done(V.tensor_scalar(T.h1[:, hs], T.lst[:, hs], 15, None, ALU.bitwise_and), "h0")
+            elif c == "B":
+                wait(V, "h0")
+                done(V.tensor_scalar(T.h2[:, hs], T.h1[:, hs], float(W - 1), None, ALU.mult), "h1")
+            elif c == "C":
+                wait(V, "h1")
+                done(V.tensor_tensor(T.h3[:, hs], T.h2[:, hs], T.lst[:, hs], ALU.add), "h2")
+            elif c == "D":
+                wait(V, "h2")
+                done(V.tensor_scalar(T.posa[:, hs], T.h3[:, hs], 1.0 / 16, None, ALU.mult), "h3")
+            elif c == "i":
+                waitd(V, "reda")
+                done(V.tensor_scalar(T.inva[:], T.reda[:], 16.25 - BASE, 0.0, ALU.add, ALU.max), "inva")
+            else:
+                waitd(V, "sa")
+                done(V.tensor_copy(T.l16[:, ca], T.lst[:, ca]), "l16a")
+
+    steps(STEPS[0])
+
+    def scans(h, src, bound, start, clamp, between=lambda: None):
+        o = 2 * h * S
+        back = slice(o + 2 * S - 2, o + S - 1, -1)
+        done(V.tensor_tensor_scan(T.fb[:, o + 1:o + S], src[:, 0:S - 1], bound[:, 0:S - 1], start, ALU.add, clamp),
+             "sf%d" % h)
+        between()
+        done(V.tensor_tensor_scan(T.fb[:, back], src[:, S - 1:0:-1], bound[:, 0:S - 1], start, ALU.add, clamp),
+             "sb%d" % h)
+
+    def scatter(lo, hi, name):
+        done(A.activation(T.win[:, 0:W].indirect(T.pos[:, lo // 16:hi // 16]), T.vals[:, lo:hi], ACT.Silu), name)
+
+    cuts = pieces(0, CUTS)
+    waitd(V, "a")
+    scans(0, T.al, T.send0, -TOP, ALU.max, lambda: steps(STEPS[1]))
+    part = lambda c: T.fb[:, "fb".index(c[0]) * S + cuts[int(c[1])][0]:"fb".index(c[0]) * S + cuts[int(c[1])][1]]
+
+    def cap(Q, c):
+        x = part(c)
+        if Q is A:
+            done(A.activation(x, x, ACT.Relu, scale=-1.0), "cap" + c)
+        else:
+            done(V.tensor_scalar(x, x, -1.0, 0.0, ALU.mult, ALU.max), "cap" + c)
+
+    wait(A, "va")
+    if NH:
+        waitd(A, "inita")
+        wait(A, "vh", "h3")
+        done(A.activation(T.wina[:, 0:W].indirect(T.posa[:, 0:NH // 16]), T.vals[:, 0:NH], ACT.Silu), "sca")
+    if N1:
+        waitd(A, "init")
+        wait(A, "vh", "p3")
+        scatter(0, N1, "sc1")
+    wait(A, "sf0")
+    for c in CAPA:
+        if c == [x for x in CAPA if x[0] == "b"][0]:
+            wait(A, "sb0")
+        cap(A, c)
+    if NH:
+        wait(P, "ident", "capf0")
+        P.matmul(T.sum2[:, 0:NH], T.ident[:], part("f0"), True, False)
+        wait(P, "capb0")
+        done(P.matmul(T.sum2[:, 0:NH], T.ident[:], part("b0"), False, True), "xsum")
+        wait(A, "xsum", "xpad")
+        done(A.activation(T.xd[:, 16:16 + NH], T.sum2[:, 0:NH], ACT.Identity, bias=TOP), "xd")
+    waitd(A, "init")
+    wait(A, "v1", "sc1" if N1 else "p3")
+    scatter(N1, S, "scb")
+    steps(STEPS[2])
+    wait(V, "sb0")
+    first = 1 if NH else 0
+    for i, (lo, hi) in list(enumerate(cuts))[first:]:
+        for c in ("f%d" % i, "b%d" % i):
+            if c not in CAPA:
+                cap(V, c)
+        steps(STEPS[3 + i])
+        wait(V, "capf%d" % i, "capb%d" % i, "e%d" % (i - 1) if i > first else "l16a")
+        done(V.tensor_tensor(T.send0[:, 0:W].indirect(T.l16[:, lcol(0, lo, hi)]), part("f%d" % i), part("b%d" % i),
+                             ALU.add), "e%d" % i)
+    last = "e%d" % (len(cuts) - 1)
+    if NH:
+        wait(V, "inva", "xd", last)
+        for r in [r for x in calls_of(rank, 0) for r, e in x] + [rank]:
+            done(V.tensor_tensor(blk(T.recv0 if r == rank else T.uu, r),
+                                 T.xd[:, 0:16 + NH].indirect(T.inva[:, r * KC:(r + 1) * KC]), blk(T.send0, r), ALU.add),
+                 "own" if r == rank else "w%d" % r)
+        for call in calls_of(rank, 0):
+            wait(g, *["w%d" % r for r, e in call])
+            send(call, T.uu, T.recv0, T.sem.arr0)
+        g.wait_ge(T.sem.sent, sent[0])
+        g.sem_inc(sem("gone"), 1)
+    else:
+        wait(g, last)
+        for call in calls_of(rank, 0):
+            send(call, T.send0, T.recv0, T.sem.arr0)
+        wait(V, last)
+        done(V.tensor_copy(blk(T.recv0, rank), blk(T.send0, rank)), "own")
+    ys0 = sum(YV)
+    if not PE:
+        g.wait_ge(T.sem.sent, sent[0])
+        dma(g.dma_start(T.y[:, ys0:S], T.al[:, ys0:S]), "pre")
+    lv = S - sum(LA)
+    done(V.tensor_copy(T.l16[:, cb], T.lst[:, cb]), "l16b")
+    done(V.memset(T.fb[:, 2 * S:4 * S:2 * S - 1], 0.0), "pad1")
+    if ZG < S:
+        done(V.memset(T.zero[:, ZG:S], 0.0), "zerov")
+        wait(V, "zerov")
+    waitd(V, "b")
+    done(V.tensor_scalar(T.bl[:, 0:lv], T.bl[:, 0:lv], TOP, None, ALU.add), "b15")
+
+    def finish():
+        waitd(V, "red")
+        done(V.tensor_scalar(T.inv[:], T.red[:], 0.25 - BASE, 0.0, ALU.add, ALU.max), "inv")
+
+    if INV == 0:
+        finish()
+
+    wait(V, "l16b", "own", "zero", "b15", "pad1")
+    V.wait_ge(T.sem.arr0, arrivals(0))
+    done(V.tensor_tensor(T.l2[:, 0:lv], T.recv0[:, 0:W].indirect(T.l16[:, lcol(1, 0, lv)]), T.bl[:, 0:lv],
+                         ALU.subtract), "l2")
+    if INV == 1:
+        finish()
+    mine = pieces(lv, LA)
+    acc = lambda i: T["sum%d" % i][:, 0:LA[i]]
+    wait(P, "ident")
+    waitd(P, "b")
+    wait(A, "l16b", "own")
+    A.wait_ge(T.sem.arr0, arrivals(0))
+    for i, (lo, hi) in enumerate(mine):
+        P.matmul(acc(i), T.ident[:], T.bl[:, lo:hi], True, False)
+        done(A.activation(T.pl[:, lo:hi], T.recv0[:, 0:W].indirect(T.l16[:, lcol(1, lo, hi)]), ACT.Identity,
+                          bias=TOP, scale=-1.0), "pl%d" % i)
+    for i, (lo, hi) in enumerate(mine):
+        wait(P, "pl%d" % i)
+        done(P.matmul(acc(i), T.ident[:], T.pl[:, lo:hi], False, True), "mm%d" % i)
+        wait(A, "mm%d" % i)
+        done(A.activation(T.l2[:, lo:hi], acc(i), ACT.Identity, scale=-1.0), "la%d" % i)
+    wait(V, "l2", *["la%d" % i for i in range(len(LA))])
+    scans(1, T.l2, T.zero, 0.0, ALU.min, finish if INV == 2 else lambda: None)
+    F, B = T.fb[:, 2 * S:3 * S], T.fb[:, 3 * S:4 * S]
+    wait(V, "sf1")
+    if VCAP:
+        c = S - VCAP
+        done(V.tensor_scalar(T.fc[:, c:S], T.fb[:, 2 * S + c:3 * S], TOP, 0.0, ALU.add, ALU.max), "cap")
+        wait(A, "sf1")
+        done(A.activation(T.fc[:, 0:c], T.fb[:, 2 * S:2 * S + c], ACT.Relu, bias=TOP), "capa")
+        wait(V, "capa")
+    else:
+        done(V.tensor_scalar(T.fc[:], F, -TOP, -1.0, ALU.max, ALU.mult), "cap")
+    calls = calls_of(rank, 1)
+    order = [r for x in calls for r, e in x] + [rank]
+    off = lambda r: T.inv[:, r * KC:(r + 1) * KC]
+    solo = order[SOLO] if SOLO is not None else None
+    wait(A, "inv")
+    if solo is not None:
+        wait(A, "sf1")
+        done(A.activation(T.uf[:], F.indirect(off(solo)), ACT.Relu, bias=TOP), "uf")
+        wait(P, "uf")
+        P.matmul(T.sum2[:, 0:CAP], T.ident[:], T.uf[:], True, False)
+        wait(P, "u%d" % solo)
+        done(P.matmul(T.sum2[:, 0:CAP], T.ident[:], blk(T.uu, solo), False, True), "both")
+    if NH:
+        wait(A, "gone")
+    wait(A, "sb1")
+    for r in order:
+        if solo is not None and r == order[EVAC]:
+            wait(A, "both")
+            done(A.activation(blk(T.send1, solo), T.sum2[:, 0:CAP], ACT.Identity, bias=TOP, scale=-1.0), "x%d" % solo)
+        done(A.activation(blk(T.uu, r), B.indirect(off(r)), ACT.Relu, bias=TOP), "u%d" % r)
+    wait(V, "inv", "cap")
+    for r in order:
+        if r != solo:
+            wait(V, "u%d" % r)
+            out = blk(T.recv1, r) if r == rank else blk(T.send1, r)
+            done(V.tensor_tensor(out, T.fc[:, 0:S].indirect(off(r)), blk(T.uu, r),
+                                 ALU.add if VCAP else ALU.subtract), "x%d" % r)
+    for k, call in enumerate(calls):
+        wait(g, *["x%d" % r for r, e in call])
+        send(call, T.send1, T.recv1, T.sem["arr1%d" % (k if VCAP else 0)])
+
+    wait(V, "x%d" % rank)
+    wait(A, "x%d" % rank, "l16a")
+    if VCAP:
+        coming = [(k, q, len(e)) for k in range(len(calls)) for q in range(N) if q != rank
+                  for r, e in calls_of(q, 1)[k] if r == rank]
+        landed = [(T.sem["arr1%d" % k], sum(n for j, q, n in coming if j == k)) for k in range(len(calls))]
+        for i, (k, q, n) in enumerate([(None, rank, 0)] + coming):
+            Q = A if i in FLIP_A else V
+            if n:
+                Q.wait_ge(*landed[k])
+            if Q is A:
+                done(A.activation(blk(T.uu, q), blk(T.recv1, q), ACT.Identity, bias=TOP, scale=-1.0), "q%d" % q)
+            else:
+                done(V.tensor_scalar(blk(T.uu, q), blk(T.recv1, q), -1.0, TOP, ALU.mult, ALU.add), "q%d" % q)
+        wait(V, *["q%d" % q for q in range(N)])
+    else:
+        landed = [(T.sem.arr10, arrivals(1))]
+        V.wait_ge(*landed[0])
+    scale, bias = (-1.0, TOP) if VCAP else (1.0, 0.0)
+    for i, (lo, hi) in enumerate(pieces(0, YV)):
+        done(V.tensor_tensor(T.yl[:, lo:hi], (T.uu if VCAP else T.recv1)[:, 0:W].indirect(T.l16[:, lcol(0, lo, hi)]),
+                             T.al[:, lo:hi], ALU.add), "yv%d" % i)
+    for x in landed:
+        A.wait_ge(*x)
+    theirs = pieces(ys0, YS)
+    for i, (lo, hi) in enumerate(theirs):
+        done(A.activation((T.pl if PE else T.yl)[:, lo:hi], T.recv1[:, 0:W].indirect(T.l16[:, lcol(0, lo, hi)]),
+                          ACT.Identity, bias=bias, scale=scale), "ya%d" % i)
+    if PE:
+        for i, (lo, hi) in enumerate(theirs):
+            wait(P, "la%d" % i)
+            P.matmul(T["sum%d" % i][:, 0:hi - lo], T.ident[:], T.al[:, lo:hi], True, False)
+        for i, (lo, hi) in enumerate(theirs):
+            wait(P, "ya%d" % i)
+            done(P.matmul(T["sum%d" % i][:, 0:hi - lo], T.ident[:], T.pl[:, lo:hi], False, True), "ym%d" % i)
+            wait(A, "ym%d" % i)
+            done(A.activation(T.yl[:, lo:hi], T["sum%d" % i][:, 0:hi - lo], ACT.Identity), "yb%d" % i)
+        for i, (lo, hi) in enumerate(theirs):
+            if "abc"[i] not in STORES:
+                wait(A, "yb%d" % i)
+                A.dma_start(T.y[:, lo:hi], T.yl[:, lo:hi]).then_inc(sem("stored"), 16)
+    else:
+        waitd(g, "pre")
+        for i, (lo, hi) in enumerate(theirs):
+            wait(g, "ya%d" % i)
+            g.dma_start(T.y[:, lo:hi], T.yl[:, lo:hi], accum_op=ALU.add).then_inc(sem("added"), 16)
         g.wait_ge(sem("added"), 16 * len(YS))
     g.wait_ge(T.sem.sent, sent[0])

from concourse.bass import DstId, RemoteDMATransfer
from concourse.mybir import AluOpType as ALU, ActivationFunctionType as ACT

N, S, CAP = 8, 2560, 384
W = N * CAP
KS, KW, KC = S // 16, W // 16, CAP // 16
BASE = 32
TOP = 15.0

LA = (448, 384)
YV = (512, 640, 544)
YS = (480, 384)
CALLS = (("FFFFNNN",), ("FF", "FN", "F", "N", "N"))
I0 = 64
CUTS = (384, 1152, 1024)
CAPA = ("f0", "f1", "b1", "f2", "b2")
LOADS = (("sb", "a", "sa", "b", "init"), ())
N1 = 0
ZG = 1280
LATE = True
STEPS = ("0123", "", "a", "", "", "", "")
INV = 1
EVAC = 7
SOLO = 5
VCAP = 0
FLIP_A = (1, 3, 5)
PE = True
STORES = "01a2"
NH = 0

SCRATCH = {
    "al": ("sbuf", [128, S], "bfloat16"),
    "bl": ("sbuf", [128, S], "bfloat16"),
    "l2": ("sbuf", [128, S], "bfloat16"),
    "pl": ("sbuf", [128, S], "bfloat16"),
    "yl": ("sbuf", [128, S], "bfloat16"),
    "zero": ("sbuf", [128, S], "bfloat16"),
    "fb": ("sbuf", [128, 4 * S], "bfloat16"),
    "fc": ("sbuf", [128, S], "bfloat16"),
    "uf": ("sbuf", [128, CAP], "bfloat16"),
    "uu": ("sbuf", [128, W], "bfloat16"),
    "send0": ("sbuf", [128, W], "bfloat16"),
    "send1": ("sbuf", [128, W], "bfloat16"),
    "recv0": ("sbuf", [128, W], "bfloat16"),
    "recv1": ("sbuf", [128, W], "bfloat16"),
    "ones": ("sbuf", [128, 128], "bfloat16"),
    "ident": ("sbuf", [128, 128], "bfloat16"),
    "vals": ("sbuf", [128, S], "float32"),
    "win": ("sbuf", [128, W], "float32"),
    "wina": ("sbuf", [128, W], "float32"),
    "reda": ("sbuf", [128, KW], "float32"),
    "inva": ("sbuf", [128, KW], "uint16"),
    "xd": ("sbuf", [128, 528], "bfloat16"),
    "h1": ("sbuf", [128, 32], "int32"),
    "h2": ("sbuf", [128, 32], "float32"),
    "h3": ("sbuf", [128, 32], "float32"),
    "posa": ("sbuf", [128, 32], "uint16"),
    "zt": ("sbuf", [128, KW], "float32"),
    "red": ("sbuf", [128, KW], "float32"),
    "inv": ("sbuf", [128, KW], "uint16"),
    "lst": ("sbuf", [128, 2 * KS], "int32"),
    "t1": ("sbuf", [128, KS], "int32"),
    "t2": ("sbuf", [128, KS], "float32"),
    "t3": ("sbuf", [128, KS], "float32"),
    "pos": ("sbuf", [128, KS], "uint16"),
    "l16": ("sbuf", [128, 2 * KS], "uint16"),
    "sum0": ("psum", [128, 512], "float32"),
    "sum1": ("psum", [128, 512], "float32"),
    "sum2": ("psum", [128, 512], "float32"),
}
POOL = 120
SEMAPHORES = ["arr0", "sent"] + ["arr1%d" % i for i in range(N)] + ["e%d" % i for i in range(POOL)]


def bits(engines):
    m = 0
    for e in engines:
        m |= 1 << e
    return m


def rank_program(g, core, T, topo):
    rank = T.rank_of(core)
    if rank is None:
        return
    V, A, Y, P = g.vector, g.scalar, g.sync, g.tensor
    names = {}

    def sem(name):
        if name not in names:
            names[name] = T.sem["e%d" % len(names)]
        return names[name]

    def done(ins, name):
        ins.then_inc(sem(name), 1)

    def dma(ins, name):
        ins.then_inc(sem(name), 16)

    def wait(q, *ns):
        for n in ns:
            q.wait_ge(sem(n), 1)

    def waitd(q, *ns):
        for n in ns:
            q.wait_ge(sem(n), 16)

    def calls_of(q, h):
        cq = T.cores[q]
        near = [r for r in range(N) if topo.die(T.cores[r]) == topo.die(cq)]
        far = [r for r in range(N) if r not in near]
        k = near.index(q)
        near = [near[(k + i) % len(near)] for i in range(1, len(near))]
        far = [far[(k + i) % len(far)] for i in range(len(far))]
        engines = lambda r: topo.engines(cq, T.cores[r])

        def deal(ranks, pick):
            n = 1 << (len(ranks) - 1).bit_length()
            share = lambda r, js: [e for j in js for e in pick(engines(r))[j::n]]
            extra = n - len(ranks)
            return [(r, share(r, (i, n - 1 - i) if i < extra else (i,))) for i, r in enumerate(ranks)]

        out = []
        for kinds in CALLS[h]:
            rs = [far.pop(0) if c in "Ff" else near.pop(0) for c in kinds]
            fs = [r for r, c in zip(rs, kinds) if c in "Ff"]
            ns = [r for r, c in zip(rs, kinds) if c in "Nn"]
            half = (fs and ns) or kinds.islower()
            dealt = dict((deal(fs, lambda e: e[0::2] if half else e) if fs else []) +
                         (deal(ns, lambda e: e[1::2] if half else e) if ns else []))
            out.append([(r, dealt[r]) for r in rs])
        return out

    def arrivals(h):
        return sum(len(e) for q in range(N) if q != rank for x in calls_of(q, h) for r, e in x if r == rank)

    blk = lambda t, r: t[:, r * CAP:(r + 1) * CAP]
    lcol = lambda h, lo, hi: slice(h * KS + lo // 16, h * KS + hi // 16)
    ca, cb = lcol(0, 0, S), lcol(1, 0, S)
    rows = T.win[0:128:16, :]
    sent = [0]

    def send(call, src, dst, arr):
        trs = []
        for r, eng in call:
            rid, pid, _ = topo.addr(T.cores[r])
            trs.append(RemoteDMATransfer(dst_ids=[DstId(rid=rid, pnc=pid)], dma_engine_mask=bits(eng),
                                         remote_sem=arr, src=blk(src, r), dst=blk(dst, rank)))
            sent[0] += len(eng)
        g.remote_dma_fused(trs, local_sem=T.sem.sent)

    def pieces(lo, sizes):
        out = []
        for n in sizes:
            out.append((lo, lo + n))
            lo += n
        return out

    loads = {"sb": T.lst[:, cb], "sa": T.lst[:, ca], "a": T.al[:], "b": T.bl[:]}
    for Q, which in zip((Y, A), LOADS):
        for name in which:
            if name == "init":
                wait(Q, "zt")
                dma(Q.dma_start(rows, T.zt[:]), "init")
            else:
                dma(Q.dma_start(loads[name], T[name][:]), name)
    if NH:
        wait(Y, "sca")
        dma(Y.dma_start(T.reda[:], T.wina[0:128:16, :]), "reda")
    wait(Y, "scb")
    if LATE:
        Y.wait_ge(T.sem.sent, sum(len(e) for x in calls_of(rank, 0) for r, e in x))
    dma(Y.dma_start(T.red[:], rows), "red")
    for c in STORES:
        i = int(c) if c.isdigit() else "abc".index(c)
        lo, hi = pieces(0, YV)[i] if c.isdigit() else pieces(sum(YV), YS)[i]
        wait(Y, ("yv%d" if c.isdigit() else "yb%d") % i)
        Y.dma_start(T.y[:, lo:hi], T.yl[:, lo:hi]).then_inc(sem("stored"), 16)
    Y.wait_ge(sem("stored"), 16 * (len(YV) + (len(YS) if PE else 0)))

    def iota(out, step, base, name):
        done(g.iota(out, [[step, out.shape[1]]], base, 0, allow_small_or_imprecise_dtypes=True), name)

    iota(T.vals[:, 0:I0], 1, BASE, "v0")
    if NH:
        done(V.memset(T.zt[:], 0.0), "zt")
        done(V.memset(T.xd[:, 0:16], 0.0), "xpad")
        wait(A, "zt")
        dma(A.dma_start(T.wina[0:128:16, :], T.zt[:]), "inita")
        iota(T.vals[:, I0:NH], 1, BASE + I0, "vh")
        iota(T.vals[:, NH:S - I0], 1, BASE + NH, "v1")
    elif N1:
        done(V.memset(T.zt[:], 0.0), "zt")
        iota(T.vals[:, I0:N1], 1, BASE + I0, "vh")
        iota(T.vals[:, N1:S - I0], 1, BASE + N1, "v1")
    else:
        iota(T.vals[:, I0:S - I0], 1, BASE + I0, "v1")
        iota(T.zt[:], 0, 0, "zt")
    iota(T.ones[:], 0, 1, "ones")
    wait(g, "ones")
    done(g.affine_select(T.ident[:], T.ones[:], [[-1, 128]], ALU.is_equal, 0.0, 0, 1), "ident")
    iota(T.zero[:, 0:ZG], 0, 0, "zero")
    done(V.memset(T.send0[:], -TOP), "clear")
    done(V.memset(T.fb[:, 0:2 * S:2 * S - 1], -TOP), "pad0")
    wait(A, "v0")
    done(A.activation(T.vals[:, S - I0:S], T.vals[:, 0:I0], ACT.Silu, bias=float(S - I0)), "va")

    wait(V, "pad0", "clear")
    hs = slice(0, NH // 16)

    def steps(which):
        for c in which:
            if c == "0":
                waitd(V, "sb")
                done(V.tensor_scalar(T.t1[:], T.lst[:, cb], 15, None, ALU.bitwise_and), "p0")
            elif c == "1":
                wait(V, "p0")
                done(V.tensor_scalar(T.t2[:], T.t1[:], float(W - 1), None, ALU.mult), "p1")
            elif c == "2":
                wait(V, "p1")
                done(V.tensor_tensor(T.t3[:], T.t2[:], T.lst[:, cb], ALU.add), "p2")
            elif c == "3":
                wait(V, "p2")
                done(V.tensor_scalar(T.pos[:], T.t3[:], 1.0 / 16, None, ALU.mult), "p3")
            elif c == "A":
                waitd(V, "sa")
                done(V.tensor_scalar(T.h1[:, hs], T.lst[:, hs], 15, None, ALU.bitwise_and), "h0")
            elif c == "B":
                wait(V, "h0")
                done(V.tensor_scalar(T.h2[:, hs], T.h1[:, hs], float(W - 1), None, ALU.mult), "h1")
            elif c == "C":
                wait(V, "h1")
                done(V.tensor_tensor(T.h3[:, hs], T.h2[:, hs], T.lst[:, hs], ALU.add), "h2")
            elif c == "D":
                wait(V, "h2")
                done(V.tensor_scalar(T.posa[:, hs], T.h3[:, hs], 1.0 / 16, None, ALU.mult), "h3")
            elif c == "i":
                waitd(V, "reda")
                done(V.tensor_scalar(T.inva[:], T.reda[:], 16.25 - BASE, 0.0, ALU.add, ALU.max), "inva")
            else:
                waitd(V, "sa")
                done(V.tensor_copy(T.l16[:, ca], T.lst[:, ca]), "l16a")

    steps(STEPS[0])

    def scans(h, src, bound, start, clamp, between=lambda: None):
        o = 2 * h * S
        back = slice(o + 2 * S - 2, o + S - 1, -1)
        done(V.tensor_tensor_scan(T.fb[:, o + 1:o + S], src[:, 0:S - 1], bound[:, 0:S - 1], start, ALU.add, clamp),
             "sf%d" % h)
        between()
        done(V.tensor_tensor_scan(T.fb[:, back], src[:, S - 1:0:-1], bound[:, 0:S - 1], start, ALU.add, clamp),
             "sb%d" % h)

    def scatter(lo, hi, name):
        done(A.activation(T.win[:, 0:W].indirect(T.pos[:, lo // 16:hi // 16]), T.vals[:, lo:hi], ACT.Silu), name)

    cuts = pieces(0, CUTS)
    waitd(V, "a")
    scans(0, T.al, T.send0, -TOP, ALU.max, lambda: steps(STEPS[1]))
    part = lambda c: T.fb[:, "fb".index(c[0]) * S + cuts[int(c[1])][0]:"fb".index(c[0]) * S + cuts[int(c[1])][1]]

    def cap(Q, c):
        x = part(c)
        if Q is A:
            done(A.activation(x, x, ACT.Relu, scale=-1.0), "cap" + c)
        else:
            done(V.tensor_scalar(x, x, -1.0, 0.0, ALU.mult, ALU.max), "cap" + c)

    wait(A, "va")
    if NH:
        waitd(A, "inita")
        wait(A, "vh", "h3")
        done(A.activation(T.wina[:, 0:W].indirect(T.posa[:, 0:NH // 16]), T.vals[:, 0:NH], ACT.Silu), "sca")
    if N1:
        waitd(A, "init")
        wait(A, "vh", "p3")
        scatter(0, N1, "sc1")
    wait(A, "sf0")
    for c in CAPA:
        if c == [x for x in CAPA if x[0] == "b"][0]:
            wait(A, "sb0")
        cap(A, c)
    if NH:
        wait(P, "ident", "capf0")
        P.matmul(T.sum2[:, 0:NH], T.ident[:], part("f0"), True, False)
        wait(P, "capb0")
        done(P.matmul(T.sum2[:, 0:NH], T.ident[:], part("b0"), False, True), "xsum")
        wait(A, "xsum", "xpad")
        done(A.activation(T.xd[:, 16:16 + NH], T.sum2[:, 0:NH], ACT.Identity, bias=TOP), "xd")
    waitd(A, "init")
    wait(A, "v1", "sc1" if N1 else "p3")
    scatter(N1, S, "scb")
    steps(STEPS[2])
    wait(V, "sb0")
    first = 1 if NH else 0
    for i, (lo, hi) in list(enumerate(cuts))[first:]:
        for c in ("f%d" % i, "b%d" % i):
            if c not in CAPA:
                cap(V, c)
        steps(STEPS[3 + i])
        wait(V, "capf%d" % i, "capb%d" % i, "e%d" % (i - 1) if i > first else "l16a")
        done(V.tensor_tensor(T.send0[:, 0:W].indirect(T.l16[:, lcol(0, lo, hi)]), part("f%d" % i), part("b%d" % i),
                             ALU.add), "e%d" % i)
    last = "e%d" % (len(cuts) - 1)
    if NH:
        wait(V, "inva", "xd", last)
        for r in [r for x in calls_of(rank, 0) for r, e in x] + [rank]:
            done(V.tensor_tensor(blk(T.recv0 if r == rank else T.uu, r),
                                 T.xd[:, 0:16 + NH].indirect(T.inva[:, r * KC:(r + 1) * KC]), blk(T.send0, r), ALU.add),
                 "own" if r == rank else "w%d" % r)
        for call in calls_of(rank, 0):
            wait(g, *["w%d" % r for r, e in call])
            send(call, T.uu, T.recv0, T.sem.arr0)
        g.wait_ge(T.sem.sent, sent[0])
        g.sem_inc(sem("gone"), 1)
    else:
        wait(g, last)
        for call in calls_of(rank, 0):
            send(call, T.send0, T.recv0, T.sem.arr0)
        wait(V, last)
        done(V.tensor_copy(blk(T.recv0, rank), blk(T.send0, rank)), "own")
    ys0 = sum(YV)
    if not PE:
        g.wait_ge(T.sem.sent, sent[0])
        dma(g.dma_start(T.y[:, ys0:S], T.al[:, ys0:S]), "pre")
    lv = S - sum(LA)
    done(V.tensor_copy(T.l16[:, cb], T.lst[:, cb]), "l16b")
    done(V.memset(T.fb[:, 2 * S:4 * S:2 * S - 1], 0.0), "pad1")
    if ZG < S:
        done(V.memset(T.zero[:, ZG:S], 0.0), "zerov")
        wait(V, "zerov")
    waitd(V, "b")
    done(V.tensor_scalar(T.bl[:, 0:lv], T.bl[:, 0:lv], TOP, None, ALU.add), "b15")

    def finish():
        waitd(V, "red")
        done(V.tensor_scalar(T.inv[:], T.red[:], 0.25 - BASE, 0.0, ALU.add, ALU.max), "inv")

    if INV == 0:
        finish()

    wait(V, "l16b", "own", "zero", "b15", "pad1")
    V.wait_ge(T.sem.arr0, arrivals(0))
    done(V.tensor_tensor(T.l2[:, 0:lv], T.recv0[:, 0:W].indirect(T.l16[:, lcol(1, 0, lv)]), T.bl[:, 0:lv],
                         ALU.subtract), "l2")
    if INV == 1:
        finish()
    mine = pieces(lv, LA)
    acc = lambda i: T["sum%d" % i][:, 0:LA[i]]
    wait(P, "ident")
    waitd(P, "b")
    wait(A, "l16b", "own")
    A.wait_ge(T.sem.arr0, arrivals(0))
    for i, (lo, hi) in enumerate(mine):
        P.matmul(acc(i), T.ident[:], T.bl[:, lo:hi], True, False)
        done(A.activation(T.pl[:, lo:hi], T.recv0[:, 0:W].indirect(T.l16[:, lcol(1, lo, hi)]), ACT.Identity,
                          bias=TOP, scale=-1.0), "pl%d" % i)
    for i, (lo, hi) in enumerate(mine):
        wait(P, "pl%d" % i)
        done(P.matmul(acc(i), T.ident[:], T.pl[:, lo:hi], False, True), "mm%d" % i)
        wait(A, "mm%d" % i)
        done(A.activation(T.l2[:, lo:hi], acc(i), ACT.Identity, scale=-1.0), "la%d" % i)
    wait(V, "l2", *["la%d" % i for i in range(len(LA))])
    scans(1, T.l2, T.zero, 0.0, ALU.min, finish if INV == 2 else lambda: None)
    F, B = T.fb[:, 2 * S:3 * S], T.fb[:, 3 * S:4 * S]
    wait(V, "sf1")
    if VCAP:
        c = S - VCAP
        done(V.tensor_scalar(T.fc[:, c:S], T.fb[:, 2 * S + c:3 * S], TOP, 0.0, ALU.add, ALU.max), "cap")
        wait(A, "sf1")
        done(A.activation(T.fc[:, 0:c], T.fb[:, 2 * S:2 * S + c], ACT.Relu, bias=TOP), "capa")
        wait(V, "capa")
    else:
        done(V.tensor_scalar(T.fc[:], F, -TOP, -1.0, ALU.max, ALU.mult), "cap")
    calls = calls_of(rank, 1)
    order = [r for x in calls for r, e in x] + [rank]
    off = lambda r: T.inv[:, r * KC:(r + 1) * KC]
    solo = order[SOLO] if SOLO is not None else None
    wait(A, "inv")
    if solo is not None:
        wait(A, "sf1")
        done(A.activation(T.uf[:], F.indirect(off(solo)), ACT.Relu, bias=TOP), "uf")
        wait(P, "uf")
        P.matmul(T.sum2[:, 0:CAP], T.ident[:], T.uf[:], True, False)
        wait(P, "u%d" % solo)
        done(P.matmul(T.sum2[:, 0:CAP], T.ident[:], blk(T.uu, solo), False, True), "both")
    if NH:
        wait(A, "gone")
    wait(A, "sb1")
    for r in order:
        if solo is not None and r == order[EVAC]:
            wait(A, "both")
            done(A.activation(blk(T.send1, solo), T.sum2[:, 0:CAP], ACT.Identity, bias=TOP, scale=-1.0), "x%d" % solo)
        done(A.activation(blk(T.uu, r), B.indirect(off(r)), ACT.Relu, bias=TOP), "u%d" % r)
    wait(V, "inv", "cap")
    for r in order:
        if r != solo:
            wait(V, "u%d" % r)
            out = blk(T.recv1, r) if r == rank else blk(T.send1, r)
            done(V.tensor_tensor(out, T.fc[:, 0:S].indirect(off(r)), blk(T.uu, r),
                                 ALU.add if VCAP else ALU.subtract), "x%d" % r)
    for k, call in enumerate(calls):
        wait(g, *["x%d" % r for r, e in call])
        send(call, T.send1, T.recv1, T.sem["arr1%d" % (k if VCAP else 0)])

    wait(V, "x%d" % rank)
    wait(A, "x%d" % rank, "l16a")
    if VCAP:
        coming = [(k, q, len(e)) for k in range(len(calls)) for q in range(N) if q != rank
                  for r, e in calls_of(q, 1)[k] if r == rank]
        landed = [(T.sem["arr1%d" % k], sum(n for j, q, n in coming if j == k)) for k in range(len(calls))]
        for i, (k, q, n) in enumerate([(None, rank, 0)] + coming):
            Q = A if i in FLIP_A else V
            if n:
                Q.wait_ge(*landed[k])
            if Q is A:
                done(A.activation(blk(T.uu, q), blk(T.recv1, q), ACT.Identity, bias=TOP, scale=-1.0), "q%d" % q)
            else:
                done(V.tensor_scalar(blk(T.uu, q), blk(T.recv1, q), -1.0, TOP, ALU.mult, ALU.add), "q%d" % q)
        wait(V, *["q%d" % q for q in range(N)])
    else:
        landed = [(T.sem.arr10, arrivals(1))]
        V.wait_ge(*landed[0])
    scale, bias = (-1.0, TOP) if VCAP else (1.0, 0.0)
    for i, (lo, hi) in enumerate(pieces(0, YV)):
        done(V.tensor_tensor(T.yl[:, lo:hi], (T.uu if VCAP else T.recv1)[:, 0:W].indirect(T.l16[:, lcol(0, lo, hi)]),
                             T.al[:, lo:hi], ALU.add), "yv%d" % i)
    for x in landed:
        A.wait_ge(*x)
    theirs = pieces(ys0, YS)
    for i, (lo, hi) in enumerate(theirs):
        done(A.activation((T.pl if PE else T.yl)[:, lo:hi], T.recv1[:, 0:W].indirect(T.l16[:, lcol(0, lo, hi)]),
                          ACT.Identity, bias=bias, scale=scale), "ya%d" % i)
    if PE:
        for i, (lo, hi) in enumerate(theirs):
            wait(P, "la%d" % i)
            P.matmul(T["sum%d" % i][:, 0:hi - lo], T.ident[:], T.al[:, lo:hi], True, False)
        for i, (lo, hi) in enumerate(theirs):
            wait(P, "ya%d" % i)
            done(P.matmul(T["sum%d" % i][:, 0:hi - lo], T.ident[:], T.pl[:, lo:hi], False, True), "ym%d" % i)
            wait(A, "ym%d" % i)
            done(A.activation(T.yl[:, lo:hi], T["sum%d" % i][:, 0:hi - lo], ACT.Identity), "yb%d" % i)
        for i, (lo, hi) in enumerate(theirs):
            if "abc"[i] not in STORES:
                wait(A, "yb%d" % i)
                A.dma_start(T.y[:, lo:hi], T.yl[:, lo:hi]).then_inc(sem("stored"), 16)
    else:
        waitd(g, "pre")
        for i, (lo, hi) in enumerate(theirs):
            wait(g, "ya%d" % i)
            g.dma_start(T.y[:, lo:hi], T.yl[:, lo:hi], accum_op=ALU.add).then_inc(sem("added"), 16)
        g.wait_ge(sem("added"), 16 * len(YS))
    g.wait_ge(T.sem.sent, sent[0])
